import numpy as np
import ml_dtypes


def mxq(x, axis, fmt="e4m3"):
    dtype, down = {"e4m3": (ml_dtypes.float8_e4m3fn, 7), "e5m2": (ml_dtypes.float8_e5m2, 14)}[fmt]
    v = np.moveaxis(np.asarray(x, np.float32).astype(ml_dtypes.bfloat16).astype(np.float64), axis, -1)
    blocks = v.reshape(v.shape[:-1] + (-1, 32))
    amax = np.abs(blocks).max(-1, keepdims=True)
    byte = np.maximum(np.where(amax > 0, np.frexp(amax)[1] - 1 + 127, 0) - down, 1)
    scale = np.exp2(byte - 127.0)
    codes = (blocks / scale).astype(np.float32).astype(dtype).astype(np.float64)
    return np.moveaxis((codes * scale).reshape(v.shape), -1, axis)


WIDE = False


def mx_kscale(k):
    if not WIDE:
        return np.ones(k)
    levels = np.array([30, -30])
    if k % 512:
        return np.exp2(np.random.permutation(np.resize(levels, k // 32))).repeat(32)
    a = np.empty((k // 512, 16))
    for p in range(k // 512):
        a[p, :8] = np.random.permutation(np.resize(levels, 8))
        for g in range(8):
            far = levels[np.abs(levels - a[p, g]) >= 10]
            a[p, g + 8] = far[np.random.randint(len(far))]
    return np.exp2(a.ravel()).repeat(32)


def f64(x):
    return np.asarray(x).astype(np.float64)


def striped(idx):
    return np.tile(np.asarray(idx).reshape(-1, 16).T, (8, 1)).astype(np.uint16)


def unstriped(offs):
    return offs[:16].T.reshape(-1).astype(np.int64)


E2M1 = np.array([0.0, 0.5, 1.0, 1.5, 2.0, 3.0, 4.0, 6.0, -0.0, -0.5, -1.0, -1.5, -2.0, -3.0, -4.0, -6.0])


def pack_weight(w, fmt):
    k, n = w.shape
    w = f64(np.asarray(w, np.float32).astype(ml_dtypes.bfloat16)).reshape(k // 32, 32, n)
    amax = np.abs(w).max(1)
    if fmt in ("e4m3", "e5m2"):
        byte = np.frexp(amax)[1] - 1 + 127 - (7 if fmt == "e4m3" else 14)
    else:
        mant, ex = np.frexp(amax / 6.0)
        byte = np.where(mant > 0.5, ex, ex - 1) + 127
    byte = np.clip(np.where(amax > 0, byte, 1), 1, 254)
    scaled = (w * np.exp2(127.0 - byte)[:, None, :]).reshape(k, n).astype(np.float32)
    by_word = np.ascontiguousarray(scaled.reshape(k // 512, 128, 4, n).transpose(0, 1, 3, 2))
    if fmt in ("e4m3", "e5m2"):
        words = by_word.astype(ml_dtypes.float8_e4m3fn if fmt == "e4m3" else ml_dtypes.float8_e5m2).view(np.uint8)
    else:
        c = by_word.astype(ml_dtypes.float4_e2m1fn).view(np.uint8) & 0xF
        words = (c[..., 0::2] | (c[..., 1::2] << 4)).reshape(k // 512, 128, 2 * n)
    return np.ascontiguousarray(words), np.ascontiguousarray(byte.astype(np.uint8).reshape(k // 512, 16, n))


def unpack_weight(words, scales, fmt):
    g, _, n = scales.shape
    words = np.ascontiguousarray(words).reshape(g, 128, n, -1)
    if fmt in ("e4m3", "e5m2"):
        vals = words.view(ml_dtypes.float8_e4m3fn if fmt == "e4m3" else ml_dtypes.float8_e5m2).astype(np.float64)
    else:
        nib = np.empty((g, 128, n, 4), np.uint8)
        nib[..., 0::2] = words & 0xF
        nib[..., 1::2] = words >> 4
        vals = E2M1[nib]
    vals = vals * np.repeat(np.exp2(scales.astype(np.float64) - 127.0), 8, axis=1)[..., None]
    return vals.transpose(0, 1, 3, 2).reshape(g * 512, n)


K, T, Z, J, R, N, E = 512, 1024, 1024, 256, 512, 256, 1024


def setup_inputs():
    n = np.random.standard_normal
    idx = np.random.permutation(T)[:J]
    idx2 = np.random.permutation(Z)[:J]
    idx3 = np.random.permutation(E)[:J]
    fk = mx_kscale(K)
    fr = mx_kscale(R)
    xtp = pack_weight(n((K, T)) / fk[:, None], "e2m1")
    xop = pack_weight(n((K, Z)) / fk[:, None], "e5m2")
    wp = pack_weight(n((K, R)) * 1 / np.sqrt(K) * fk[:, None] * fr, "e5m2")
    w2p = pack_weight(n((K, R)) * 1 / np.sqrt(K) * fk[:, None] * fr, "e4m3")
    wbp = pack_weight(n((R, N)) * 1 / np.sqrt(R) / fr[:, None], "e4m3")
    return {
        "xt_words": xtp[0],
        "xt_scales": xtp[1],
        "xo_words": xop[0],
        "xo_scales": xop[1],
        "w_words": wp[0],
        "w_scales": wp[1],
        "w2_words": w2p[0],
        "w2_scales": w2p[1],
        "wb_words": wbp[0],
        "wb_scales": wbp[1],
        "offs": striped(idx),
        "offs2": striped(idx2),
        "offs3": striped(idx3),
    }


def reference(xt_words, xt_scales, xo_words, xo_scales, w_words, w_scales, w2_words, w2_scales, wb_words, wb_scales, offs, offs2, offs3):
    idx = unstriped(offs)
    idx2 = unstriped(offs2)
    idx3 = unstriped(offs3)
    xtu = unpack_weight(xt_words, xt_scales, "e2m1")
    xou = unpack_weight(xo_words, xo_scales, "e5m2")
    wu = unpack_weight(w_words, w_scales, "e5m2")
    w2u = unpack_weight(w2_words, w2_scales, "e4m3")
    wbu = unpack_weight(wb_words, wb_scales, "e4m3")
    xtidxg = xtu[:, idx]
    xoidx2g = xou[:, idx2]
    a = wu.T @ xtidxg + w2u.T @ xoidx2g
    b = w2u.T @ xtidxg + wu.T @ xoidx2g
    hid = np.abs(a - b)
    hidq = mxq(hid, 0, "e5m2")
    p = wbu.T @ hidq
    y = np.zeros((N, E))
    y[:, idx3] = p
    return y

@@ -1,0 +1,173 @@
+from contextlib import ExitStack
+
+import concourse.mybir as mybir
+
+K, T, Z, J, R, N, E = 512, 1024, 1024, 256, 512, 256, 1024
+FLOPS = 4 * 2 * K * R * J + 2 * R * N * J
+
+F32 = mybir.dt.float32
+BF16 = mybir.dt.bfloat16
+I32 = mybir.dt.int32
+U32 = mybir.dt.uint32
+U16 = mybir.dt.uint16
+U8 = mybir.dt.uint8
+E2M1 = mybir.dt.float4_e2m1fn_x4
+E4M3 = mybir.dt.float8_e4m3fn_x4
+E5M2 = mybir.dt.float8_e5m2_x4
+ACT = mybir.ActivationFunctionType
+ALU = mybir.AluOpType
+
+P = 128
+PACK = 4
+HALF = 128
+HALVES = J // HALF
+LIST_COLS = HALF // 16
+ODD = E // 2 + 1
+
+
+def load_scale_rows(queue, plane, scales):
+    for q in range(4):
+        queue.dma_start(
+            out=plane[32 * q : 32 * q + 4, :].bitcast(I32),
+            in_=scales[0, 4 * q : 4 * q + 4, :].bitcast(I32),
+        )
+
+
+def fp8_words(words):
+    return words[0].rearrange("p n t -> p (n t)").bitcast(I32)
+
+
+def tile_list_crossed_direct_one_scattered_kernel(
+    tc, xt_words, xt_scales, xo_words, xo_scales, w_words, w_scales, w2_words, w2_scales,
+    wb_words, wb_scales, offs, offs2, offs3, out,
+):
+    nc = tc.nc
+    with ExitStack() as ctx:
+        keep = ctx.enter_context(tc.tile_pool(name="keep", bufs=1))
+        psum = ctx.enter_context(tc.psum_pool(name="psum", bufs=1))
+
+        def tile(name, shape, dtype):
+            return keep.tile(shape, dtype, name=name, align_bytes=64)
+
+        list_t = tile("list_t", [P, J // 16], U16)
+        list_o = tile("list_o", [P, J // 16], U16)
+        list_e = tile("list_e", [P, J // 16], U16)
+        xt_w = tile("xt_w", [P, T], U16)
+        xt_s = tile("xt_s", [P, T], U8)
+        xo_w = tile("xo_w", [P, Z], U32)
+        xo_s = tile("xo_s", [P, Z], U8)
+        w_w = tile("w_w", [P, R], U32)
+        w_s = tile("w_s", [P, R], U8)
+        w2_w = tile("w2_w", [P, R], U32)
+        w2_s = tile("w2_s", [P, R], U8)
+        wb_w = tile("wb_w", [P, N], U32)
+        wb_s = tile("wb_s", [P, N], U8)
+        pages = [tile("page%d" % i, [P, E], F32) for i in range(N // P)]
+
+        for plane in (xt_s, xo_s, w_s, w2_s, wb_s):
+            nc.vector.memset(plane[:].bitcast(I32), 0)
+        for page in pages:
+            nc.vector.memset(page[:, :ODD], 0.0)
+            nc.vector.memset(page[:, ODD:], 0.0)
+
+        nc.gpsimd.dma_start(out=xo_w[:].bitcast(I32), in_=fp8_words(xo_words))
+        nc.gpsimd.dma_start(out=w_w[:].bitcast(I32), in_=fp8_words(w_words))
+        nc.gpsimd.dma_start(out=w2_w[:].bitcast(I32), in_=fp8_words(w2_words))
+        nc.gpsimd.dma_start(out=wb_w[:].bitcast(I32), in_=fp8_words(wb_words))
+        nc.sync.dma_start(list_t[:], offs)
+        nc.sync.dma_start(list_o[:], offs2)
+        nc.sync.dma_start(list_e[:], offs3)
+        nc.sync.dma_start(out=xt_w[:].bitcast(I32), in_=xt_words[0].bitcast(I32))
+        load_scale_rows(nc.sync, xt_s, xt_scales)
+        load_scale_rows(nc.sync, xo_s, xo_scales)
+        load_scale_rows(nc.sync, w_s, w_scales)
+        load_scale_rows(nc.sync, w2_s, w2_scales)
+        load_scale_rows(nc.sync, wb_s, wb_scales)
+
+        def dealt(name, words, plane):
+            words_d = tile(name + "_wd", [P, PACK, P], U32)
+            plane_d = tile(name + "_sd", [P, PACK, P], U8)
+            nc.vector.tensor_copy(
+                out=plane_d[:].rearrange("p t (c i) -> p c t i", i=16),
+                in_=plane[:].rearrange("p (c i t) -> p c t i", i=16, t=PACK),
+            )
+            nc.scalar.copy(
+                out=words_d[:].rearrange("p t (c i) -> p c t i", i=4),
+                in_=words[:].rearrange("p (c i t) -> p c t i", i=4, t=PACK),
+            )
+            return words_d, plane_d
+
+        gt_w = tile("gt_w", [P, J], U16)
+        gt_s = tile("gt_s", [P, J], U8)
+        go_w = tile("go_w", [P, J], U32)
+        go_s = tile("go_s", [P, J], U8)
+        nc.vector.tensor_copy(gt_w[:], xt_w[:].indirect(list_t[:]))
+        nc.vector.tensor_copy(gt_s[:], xt_s[:].indirect(list_t[:]))
+        nc.vector.tensor_copy(go_w[:], xo_w[:].indirect(list_o[:]))
+        nc.vector.tensor_copy(go_s[:], xo_s[:].indirect(list_o[:]))
+        w_wd, w_sd = dealt("w", w_w, w_s)
+        w2_wd, w2_sd = dealt("w2", w2_w, w2_s)
+
+        first = (w_wd, w_sd, E5M2)
+        second = (w2_wd, w2_sd, E4M3)
+        bank_a = [psum.tile([P, PACK, HALF], F32, name="bank_a%d" % h) for h in range(HALVES)]
+        bank_b = [psum.tile([P, PACK, HALF], F32, name="bank_b%d" % h) for h in range(HALVES)]
+
+        def passes(bank, weight, rhs, rhs_scale, opens):
+            words_d, plane_d, fmt = weight
+            for t in range(PACK):
+                nc.tensor.matmul_mx(
+                    out=bank[:, t, :],
+                    lhsT=words_d[:, t, :].bitcast(fmt),
+                    lhsT_scale=plane_d[:, t, :],
+                    rhs=rhs,
+                    rhs_scale=rhs_scale,
+                    start=(opens and t == 0),
+                    stop=(not opens and t == PACK - 1),
+                )
+
+        cols = [slice(h * HALF, (h + 1) * HALF) for h in range(HALVES)]
+        tokens = [(gt_w[:, c].bitcast(E2M1), gt_s[:, c]) for c in cols]
+        notes = [(go_w[:, c].bitcast(E5M2), go_s[:, c]) for c in cols]
+        for banks, moving in ((bank_a, tokens), (bank_b, notes)):
+            for h in range(HALVES):
+                passes(banks[h], first, *moving[h], True)
+        for h in range(HALVES):
+            for banks, moving in ((bank_b, tokens), (bank_a, notes)):
+                passes(banks[h], second, *moving[h], False)
+
+        for h in range(HALVES):
+            b_sb = tile("b_sb%d" % h, [P, HALF, PACK], F32)
+            diff = tile("diff%d" % h, [P, HALF, PACK], F32)
+            hid = tile("hid%d" % h, [P, HALF * PACK], BF16)
+            hid_w = tile("hid_w%d" % h, [P, HALF], U32)
+            hid_s = tile("hid_s%d" % h, [P, HALF], U8)
+            nc.scalar.copy(out=b_sb[:], in_=bank_b[h][:].rearrange("p t j -> p j t"))
+            nc.vector.tensor_tensor(
+                out=diff[:], in0=bank_a[h][:].rearrange("p t j -> p j t"), in1=b_sb[:], op=ALU.subtract
+            )
+            nc.scalar.activation(out=hid[:], in_=diff[:].rearrange("p j t -> p (j t)"), func=ACT.Abs)
+            nc.vector.quantize_mx(out=hid_w[:].bitcast(E5M2), scales=hid_s[:], in_=hid[:])
+            for i, page in enumerate(pages):
+                n_cols = slice(i * P, (i + 1) * P)
+                bank_p = psum.tile([P, HALF], F32, name="bank_p%d_%d" % (h, i))
+                nc.tensor.matmul_mx(
+                    out=bank_p[:],
+                    lhsT=wb_w[:, n_cols].bitcast(E4M3),
+                    lhsT_scale=wb_s[:, n_cols],
+                    rhs=hid_w[:].bitcast(E5M2),
+                    rhs_scale=hid_s[:],
+                    start=True,
+                    stop=True,
+                )
+                p_sb = tile("p_sb%d_%d" % (h, i), [P, HALF], F32)
+                places = page[:].indirect(list_e[:, h * LIST_COLS : (h + 1) * LIST_COLS])
+                if i == 0:
+                    nc.vector.tensor_copy(out=p_sb[:], in_=bank_p[:])
+                    nc.vector.tensor_copy(out=places, in_=p_sb[:])
+                else:
+                    nc.scalar.copy(out=p_sb[:], in_=bank_p[:])
+                    nc.scalar.activation(out=places, in_=p_sb[:], func=ACT.Copy)
+
+        nc.sync.dma_start(out=out[0:P, :], in_=pages[0][:])
+        nc.scalar.dma_start(out=out[P : 2 * P, :], in_=pages[1][:])

@@ -25,8 +25,8 @@ LIST_COLS = HALF // 16
 ODD = E // 2 + 1
 
 
-def load_scale_rows(queue, plane, scales):
-    for q in range(4):
+def load_scale_rows(queues, plane, scales):
+    for q, queue in enumerate(queues):
         queue.dma_start(
             out=plane[32 * q : 32 * q + 4, :].bitcast(I32),
             in_=scales[0, 4 * q : 4 * q + 4, :].bitcast(I32),
@@ -46,46 +46,45 @@ def tile_list_crossed_direct_one_scattered_kernel(
         keep = ctx.enter_context(tc.tile_pool(name="keep", bufs=1))
         psum = ctx.enter_context(tc.psum_pool(name="psum", bufs=1))
 
-        def tile(name, shape, dtype):
-            return keep.tile(shape, dtype, name=name, align_bytes=64)
+        def tile(name, shape, dtype, tag=""):
+            return keep.tile(shape, dtype, name=name, tag=tag, align_bytes=64)
 
         list_t = tile("list_t", [P, J // 16], U16)
         list_o = tile("list_o", [P, J // 16], U16)
         list_e = tile("list_e", [P, J // 16], U16)
         xt_w = tile("xt_w", [P, T], U16)
-        xt_s = tile("xt_s", [P, T], U8)
+        xt_s = tile("xt_s", [P, T], U8, tag="token_scales_then_notes")
         xo_w = tile("xo_w", [P, Z], U32)
-        xo_s = tile("xo_s", [P, Z], U8)
-        w_w = tile("w_w", [P, R], U32)
+        xo_s = tile("xo_s", [P, Z], U8, tag="note_scales_then_page")
+        w_w = tile("w_w", [P, R], U32, tag="w_then_dealt_w2")
         w_s = tile("w_s", [P, R], U8)
         w2_w = tile("w2_w", [P, R], U32)
         w2_s = tile("w2_s", [P, R], U8)
         wb_w = tile("wb_w", [P, N], U32)
         wb_s = tile("wb_s", [P, N], U8)
-        pages = [tile("page%d" % i, [P, E], F32) for i in range(N // P)]
+        page0 = tile("page0", [P, E], F32)
 
-        for plane in (xt_s, xo_s, w_s, w2_s, wb_s):
+        for plane in (w_s, xt_s, w2_s, xo_s, wb_s):
             nc.vector.memset(plane[:].bitcast(I32), 0)
-        for page in pages:
-            nc.vector.memset(page[:, :ODD], 0.0)
-            nc.vector.memset(page[:, ODD:], 0.0)
+        nc.vector.memset(page0[:, :ODD], 0.0)
+        nc.vector.memset(page0[:, ODD:], 0.0)
 
         nc.gpsimd.dma_start(out=xo_w[:].bitcast(I32), in_=fp8_words(xo_words))
-        nc.gpsimd.dma_start(out=w_w[:].bitcast(I32), in_=fp8_words(w_words))
         nc.gpsimd.dma_start(out=w2_w[:].bitcast(I32), in_=fp8_words(w2_words))
-        nc.gpsimd.dma_start(out=wb_w[:].bitcast(I32), in_=fp8_words(wb_words))
         nc.sync.dma_start(list_t[:], offs)
         nc.sync.dma_start(list_o[:], offs2)
         nc.sync.dma_start(list_e[:], offs3)
         nc.sync.dma_start(out=xt_w[:].bitcast(I32), in_=xt_words[0].bitcast(I32))
-        load_scale_rows(nc.sync, xt_s, xt_scales)
-        load_scale_rows(nc.sync, xo_s, xo_scales)
-        load_scale_rows(nc.sync, w_s, w_scales)
-        load_scale_rows(nc.sync, w2_s, w2_scales)
-        load_scale_rows(nc.sync, wb_s, wb_scales)
+        nc.sync.dma_start(out=w_w[:].bitcast(I32), in_=fp8_words(w_words))
+        load_scale_rows([nc.sync] * 4, w_s, w_scales)
+        load_scale_rows([nc.sync] * 4, xt_s, xt_scales)
+        load_scale_rows([nc.sync] * 4, w2_s, w2_scales)
+        load_scale_rows([nc.gpsimd, nc.gpsimd, nc.sync, nc.sync], xo_s, xo_scales)
+        load_scale_rows([nc.sync] * 4, wb_s, wb_scales)
+        nc.gpsimd.dma_start(out=wb_w[:].bitcast(I32), in_=fp8_words(wb_words))
 
-        def dealt(name, words, plane):
-            words_d = tile(name + "_wd", [P, PACK, P], U32)
+        def dealt(name, words, plane, tag=""):
+            words_d = tile(name + "_wd", [P, PACK, P], U32, tag=tag)
             plane_d = tile(name + "_sd", [P, PACK, P], U8)
             nc.vector.tensor_copy(
                 out=plane_d[:].rearrange("p t (c i) -> p c t i", i=16),
@@ -97,16 +96,22 @@ def tile_list_crossed_direct_one_scattered_kernel(
             )
             return words_d, plane_d
 
+        cols = [slice(h * HALF, (h + 1) * HALF) for h in range(HALVES)]
         gt_w = tile("gt_w", [P, J], U16)
         gt_s = tile("gt_s", [P, J], U8)
-        go_w = tile("go_w", [P, J], U32)
-        go_s = tile("go_s", [P, J], U8)
+        go_s = [tile("go_s%d" % h, [P, HALF], U8) for h in range(HALVES)]
+        w_wd, w_sd = dealt("w", w_w, w_s)
         nc.vector.tensor_copy(gt_w[:], xt_w[:].indirect(list_t[:]))
         nc.vector.tensor_copy(gt_s[:], xt_s[:].indirect(list_t[:]))
+        go_w = tile("go_w", [P, J], U32, tag="token_scales_then_notes")
         nc.vector.tensor_copy(go_w[:], xo_w[:].indirect(list_o[:]))
-        nc.vector.tensor_copy(go_s[:], xo_s[:].indirect(list_o[:]))
-        w_wd, w_sd = dealt("w", w_w, w_s)
-        w2_wd, w2_sd = dealt("w2", w2_w, w2_s)
+        w2_wd, w2_sd = dealt("w2", w2_w, w2_s, tag="w_then_dealt_w2")
+        for h in range(HALVES):
+            entries = list_o[:, h * LIST_COLS : (h + 1) * LIST_COLS]
+            nc.vector.tensor_copy(go_s[h][:], xo_s[:].indirect(entries))
+        page1 = tile("page1", [P, E], F32, tag="note_scales_then_page")
+        nc.vector.memset(page1[:], 0.0)
+        pages = [page0, page1]
 
         first = (w_wd, w_sd, E5M2)
         second = (w2_wd, w2_sd, E4M3)
@@ -126,28 +131,36 @@ def tile_list_crossed_direct_one_scattered_kernel(
                     stop=(not opens and t == PACK - 1),
                 )
 
-        cols = [slice(h * HALF, (h + 1) * HALF) for h in range(HALVES)]
         tokens = [(gt_w[:, c].bitcast(E2M1), gt_s[:, c]) for c in cols]
-        notes = [(go_w[:, c].bitcast(E5M2), go_s[:, c]) for c in cols]
-        for banks, moving in ((bank_a, tokens), (bank_b, notes)):
-            for h in range(HALVES):
-                passes(banks[h], first, *moving[h], True)
-        for h in range(HALVES):
-            for banks, moving in ((bank_b, tokens), (bank_a, notes)):
-                passes(banks[h], second, *moving[h], False)
+        notes = [(go_w[:, cols[h]].bitcast(E5M2), go_s[h][:]) for h in range(HALVES)]
+        passes(bank_a[0], first, *tokens[0], True)
+        passes(bank_a[1], first, *tokens[1], True)
+        passes(bank_b[0], second, *tokens[0], True)
+        passes(bank_b[0], first, *notes[0], False)
+        passes(bank_a[0], second, *notes[0], False)
+        passes(bank_b[1], first, *notes[1], True)
+        passes(bank_b[1], second, *tokens[1], False)
+        passes(bank_a[1], second, *notes[1], False)
 
+        hid_w, hid_s = [], []
         for h in range(HALVES):
             b_sb = tile("b_sb%d" % h, [P, HALF, PACK], F32)
-            diff = tile("diff%d" % h, [P, HALF, PACK], F32)
-            hid = tile("hid%d" % h, [P, HALF * PACK], BF16)
-            hid_w = tile("hid_w%d" % h, [P, HALF], U32)
-            hid_s = tile("hid_s%d" % h, [P, HALF], U8)
+            diff = tile("diff%d" % h, [P, HALF, PACK], F32, tag="diff%d" % h)
+            hid = tile("hid%d" % h, [P, HALF * PACK], BF16, tag="hid%d" % h)
+            hid_w.append(tile("hid_w%d" % h, [P, HALF], U32))
+            hid_s.append(tile("hid_s%d" % h, [P, HALF], U8))
             nc.scalar.copy(out=b_sb[:], in_=bank_b[h][:].rearrange("p t j -> p j t"))
             nc.vector.tensor_tensor(
                 out=diff[:], in0=bank_a[h][:].rearrange("p t j -> p j t"), in1=b_sb[:], op=ALU.subtract
             )
             nc.scalar.activation(out=hid[:], in_=diff[:].rearrange("p j t -> p (j t)"), func=ACT.Abs)
-            nc.vector.quantize_mx(out=hid_w[:].bitcast(E5M2), scales=hid_s[:], in_=hid[:])
+            nc.vector.quantize_mx(out=hid_w[h][:].bitcast(E5M2), scales=hid_s[h][:], in_=hid[:])
+
+        p_sb = [
+            tile("p_sb0", [P, J], F32, tag="hid%d" % (HALVES - 1)),
+            tile("p_sb1", [P, J], F32, tag="diff%d" % (HALVES - 1)),
+        ]
+        for h in range(HALVES):
             for i, page in enumerate(pages):
                 n_cols = slice(i * P, (i + 1) * P)
                 bank_p = psum.tile([P, HALF], F32, name="bank_p%d_%d" % (h, i))
@@ -155,19 +168,19 @@ def tile_list_crossed_direct_one_scattered_kernel(
                     out=bank_p[:],
                     lhsT=wb_w[:, n_cols].bitcast(E4M3),
                     lhsT_scale=wb_s[:, n_cols],
-                    rhs=hid_w[:].bitcast(E5M2),
-                    rhs_scale=hid_s[:],
+                    rhs=hid_w[h][:].bitcast(E5M2),
+                    rhs_scale=hid_s[h][:],
                     start=True,
                     stop=True,
                 )
-                p_sb = tile("p_sb%d_%d" % (h, i), [P, HALF], F32)
+                values = p_sb[i][:, cols[h]]
                 places = page[:].indirect(list_e[:, h * LIST_COLS : (h + 1) * LIST_COLS])
                 if i == 0:
-                    nc.vector.tensor_copy(out=p_sb[:], in_=bank_p[:])
-                    nc.vector.tensor_copy(out=places, in_=p_sb[:])
+                    nc.vector.tensor_copy(out=values, in_=bank_p[:])
+                    nc.vector.tensor_copy(out=places, in_=values)
                 else:
-                    nc.scalar.copy(out=p_sb[:], in_=bank_p[:])
-                    nc.scalar.activation(out=places, in_=p_sb[:], func=ACT.Copy)
+                    nc.scalar.copy(out=values, in_=bank_p[:])
+                    nc.scalar.activation(out=places, in_=values, func=ACT.Copy)
 
         nc.sync.dma_start(out=out[0:P, :], in_=pages[0][:])
         nc.scalar.dma_start(out=out[P : 2 * P, :], in_=pages[1][:])

@@ -19,17 +19,23 @@ ALU = mybir.AluOpType
 
 P = 128
 PACK = 4
+QUADRANTS = 4
+LIVE_ROWS = 4
+LIST_ROWS = 16
 HALF = 128
 HALVES = J // HALF
-LIST_COLS = HALF // 16
+LIST_COLS = HALF // LIST_ROWS
+RUNS = (slice(0, HALF // 2), slice(HALF // 2, HALF))
 ODD = E // 2 + 1
 
 
-def load_scale_rows(queues, plane, scales):
-    for q, queue in enumerate(queues):
+def load_plane(queue, plane, scales):
+    rows_per_quadrant = P // QUADRANTS
+    for q in range(QUADRANTS):
+        rows = scales[0, LIVE_ROWS * q : LIVE_ROWS * (q + 1), :].bitcast(I32)
         queue.dma_start(
-            out=plane[32 * q : 32 * q + 4, :].bitcast(I32),
-            in_=scales[0, 4 * q : 4 * q + 4, :].bitcast(I32),
+            out=plane[rows_per_quadrant * q : rows_per_quadrant * (q + 1), :].bitcast(I32),
+            in_=rows.unsqueeze(0).broadcast_to([rows_per_quadrant // LIVE_ROWS, LIVE_ROWS, rows.shape[1]]),
         )
 
 
@@ -49,42 +55,41 @@ def tile_list_crossed_direct_one_scattered_kernel(
         def tile(name, shape, dtype, tag=""):
             return keep.tile(shape, dtype, name=name, tag=tag, align_bytes=64)
 
-        list_t = tile("list_t", [P, J // 16], U16)
-        list_o = tile("list_o", [P, J // 16], U16)
-        list_e = tile("list_e", [P, J // 16], U16)
+        list_t = tile("list_t", [P, J // LIST_ROWS], U16)
+        list_o = tile("list_o", [P, J // LIST_ROWS], U16)
+        list_e = tile("list_e", [P, J // LIST_ROWS], U16)
         xt_w = tile("xt_w", [P, T], U16)
-        xt_s = tile("xt_s", [P, T], U8, tag="token_scales_then_notes")
+        xt_s = tile("xt_s", [P, T], U8)
         xo_w = tile("xo_w", [P, Z], U32)
-        xo_s = tile("xo_s", [P, Z], U8, tag="note_scales_then_page")
-        w_w = tile("w_w", [P, R], U32, tag="w_then_dealt_w2")
+        xo_s = tile("xo_s", [P, Z], U8)
+        w_w = tile("w_w", [P, R], U32)
         w_s = tile("w_s", [P, R], U8)
         w2_w = tile("w2_w", [P, R], U32)
         w2_s = tile("w2_s", [P, R], U8)
         wb_w = tile("wb_w", [P, N], U32)
         wb_s = tile("wb_s", [P, N], U8)
-        page0 = tile("page0", [P, E], F32)
+        pages = [tile("page%d" % i, [P, E], F32) for i in range(N // P)]
 
-        for plane in (w_s, xt_s, w2_s, xo_s, wb_s):
-            nc.vector.memset(plane[:].bitcast(I32), 0)
-        nc.vector.memset(page0[:, :ODD], 0.0)
-        nc.vector.memset(page0[:, ODD:], 0.0)
+        for page in pages:
+            nc.vector.memset(page[:, :ODD], 0.0)
+            nc.vector.memset(page[:, ODD:], 0.0)
 
-        nc.gpsimd.dma_start(out=xo_w[:].bitcast(I32), in_=fp8_words(xo_words))
+        nc.gpsimd.dma_start(out=w_w[:].bitcast(I32), in_=fp8_words(w_words))
         nc.gpsimd.dma_start(out=w2_w[:].bitcast(I32), in_=fp8_words(w2_words))
-        nc.sync.dma_start(list_t[:], offs)
-        nc.sync.dma_start(list_o[:], offs2)
-        nc.sync.dma_start(list_e[:], offs3)
-        nc.sync.dma_start(out=xt_w[:].bitcast(I32), in_=xt_words[0].bitcast(I32))
-        nc.sync.dma_start(out=w_w[:].bitcast(I32), in_=fp8_words(w_words))
-        load_scale_rows([nc.sync] * 4, w_s, w_scales)
-        load_scale_rows([nc.sync] * 4, xt_s, xt_scales)
-        load_scale_rows([nc.sync] * 4, w2_s, w2_scales)
-        load_scale_rows([nc.gpsimd, nc.gpsimd, nc.sync, nc.sync], xo_s, xo_scales)
-        load_scale_rows([nc.sync] * 4, wb_s, wb_scales)
         nc.gpsimd.dma_start(out=wb_w[:].bitcast(I32), in_=fp8_words(wb_words))
+        nc.sync.dma_start(list_t[:], offs)
+        load_plane(nc.sync, w_s, w_scales)
+        nc.sync.dma_start(out=xt_w[:].bitcast(I32), in_=xt_words[0].bitcast(I32))
+        load_plane(nc.sync, xt_s, xt_scales)
+        nc.sync.dma_start(list_o[:], offs2)
+        load_plane(nc.sync, w2_s, w2_scales)
+        nc.sync.dma_start(out=xo_w[:].bitcast(I32), in_=fp8_words(xo_words))
+        load_plane(nc.sync, xo_s, xo_scales)
+        load_plane(nc.sync, wb_s, wb_scales)
+        nc.sync.dma_start(list_e[:], offs3)
 
-        def dealt(name, words, plane, tag=""):
-            words_d = tile(name + "_wd", [P, PACK, P], U32, tag=tag)
+        def dealt(name, words, plane):
+            words_d = tile(name + "_wd", [P, PACK, P], U32)
             plane_d = tile(name + "_sd", [P, PACK, P], U8)
             nc.vector.tensor_copy(
                 out=plane_d[:].rearrange("p t (c i) -> p c t i", i=16),
@@ -96,6 +101,9 @@ def tile_list_crossed_direct_one_scattered_kernel(
             )
             return words_d, plane_d
 
+        def entries(offsets, h):
+            return offsets[:, h * LIST_COLS : (h + 1) * LIST_COLS]
+
         cols = [slice(h * HALF, (h + 1) * HALF) for h in range(HALVES)]
         gt_w = tile("gt_w", [P, J], U16)
         gt_s = tile("gt_s", [P, J], U8)
@@ -103,15 +111,11 @@ def tile_list_crossed_direct_one_scattered_kernel(
         w_wd, w_sd = dealt("w", w_w, w_s)
         nc.vector.tensor_copy(gt_w[:], xt_w[:].indirect(list_t[:]))
         nc.vector.tensor_copy(gt_s[:], xt_s[:].indirect(list_t[:]))
-        go_w = tile("go_w", [P, J], U32, tag="token_scales_then_notes")
+        w2_wd, w2_sd = dealt("w2", w2_w, w2_s)
+        go_w = tile("go_w", [P, J], U32)
         nc.vector.tensor_copy(go_w[:], xo_w[:].indirect(list_o[:]))
-        w2_wd, w2_sd = dealt("w2", w2_w, w2_s, tag="w_then_dealt_w2")
         for h in range(HALVES):
-            entries = list_o[:, h * LIST_COLS : (h + 1) * LIST_COLS]
-            nc.vector.tensor_copy(go_s[h][:], xo_s[:].indirect(entries))
-        page1 = tile("page1", [P, E], F32, tag="note_scales_then_page")
-        nc.vector.memset(page1[:], 0.0)
-        pages = [page0, page1]
+            nc.vector.tensor_copy(go_s[h][:], xo_s[:].indirect(entries(list_o, h)))
 
         first = (w_wd, w_sd, E5M2)
         second = (w2_wd, w2_sd, E4M3)
@@ -133,28 +137,33 @@ def tile_list_crossed_direct_one_scattered_kernel(
 
         tokens = [(gt_w[:, c].bitcast(E2M1), gt_s[:, c]) for c in cols]
         notes = [(go_w[:, cols[h]].bitcast(E5M2), go_s[h][:]) for h in range(HALVES)]
-        passes(bank_a[0], first, *tokens[0], True)
-        passes(bank_a[1], first, *tokens[1], True)
-        passes(bank_b[0], second, *tokens[0], True)
-        passes(bank_b[0], first, *notes[0], False)
-        passes(bank_a[0], second, *notes[0], False)
-        passes(bank_b[1], first, *notes[1], True)
-        passes(bank_b[1], second, *tokens[1], False)
-        passes(bank_a[1], second, *notes[1], False)
+        for banks, weight in ((bank_a, first), (bank_b, second)):
+            for h in range(HALVES):
+                passes(banks[h], weight, *tokens[h], True)
+        for h in range(HALVES):
+            for banks, weight in ((bank_b, first), (bank_a, second)):
+                passes(banks[h], weight, *notes[h], False)
 
         hid_w, hid_s = [], []
         for h in range(HALVES):
             b_sb = tile("b_sb%d" % h, [P, HALF, PACK], F32)
             diff = tile("diff%d" % h, [P, HALF, PACK], F32, tag="diff%d" % h)
-            hid = tile("hid%d" % h, [P, HALF * PACK], BF16, tag="hid%d" % h)
+            hid = tile("hid%d" % h, [P, HALF, PACK], BF16, tag="hid%d" % h)
             hid_w.append(tile("hid_w%d" % h, [P, HALF], U32))
             hid_s.append(tile("hid_s%d" % h, [P, HALF], U8))
-            nc.scalar.copy(out=b_sb[:], in_=bank_b[h][:].rearrange("p t j -> p j t"))
-            nc.vector.tensor_tensor(
-                out=diff[:], in0=bank_a[h][:].rearrange("p t j -> p j t"), in1=b_sb[:], op=ALU.subtract
+            for s in RUNS:
+                nc.scalar.copy(out=b_sb[:, s, :], in_=bank_b[h][:, :, s].rearrange("p t j -> p j t"))
+            for s in RUNS:
+                nc.vector.tensor_tensor(
+                    out=diff[:, s, :],
+                    in0=bank_a[h][:, :, s].rearrange("p t j -> p j t"),
+                    in1=b_sb[:, s, :],
+                    op=ALU.subtract,
+                )
+                nc.scalar.activation(out=hid[:, s, :], in_=diff[:, s, :], func=ACT.Abs)
+            nc.vector.quantize_mx(
+                out=hid_w[h][:].bitcast(E5M2), scales=hid_s[h][:], in_=hid[:].rearrange("p j t -> p (j t)")
             )
-            nc.scalar.activation(out=hid[:], in_=diff[:].rearrange("p j t -> p (j t)"), func=ACT.Abs)
-            nc.vector.quantize_mx(out=hid_w[h][:].bitcast(E5M2), scales=hid_s[h][:], in_=hid[:])
 
         p_sb = [
             tile("p_sb0", [P, J], F32, tag="hid%d" % (HALVES - 1)),
@@ -174,7 +183,7 @@ def tile_list_crossed_direct_one_scattered_kernel(
                     stop=True,
                 )
                 values = p_sb[i][:, cols[h]]
-                places = page[:].indirect(list_e[:, h * LIST_COLS : (h + 1) * LIST_COLS])
+                places = page[:].indirect(entries(list_e, h))
                 if i == 0:
                     nc.vector.tensor_copy(out=values, in_=bank_p[:])
                     nc.vector.tensor_copy(out=places, in_=values)

from contextlib import ExitStack

import concourse.mybir as mybir

K, T, Z, J, R, N, E = 512, 1024, 1024, 256, 512, 256, 1024
FLOPS = 4 * 2 * K * R * J + 2 * R * N * J

F32 = mybir.dt.float32
BF16 = mybir.dt.bfloat16
I32 = mybir.dt.int32
U32 = mybir.dt.uint32
U16 = mybir.dt.uint16
U8 = mybir.dt.uint8
E2M1 = mybir.dt.float4_e2m1fn_x4
E4M3 = mybir.dt.float8_e4m3fn_x4
E5M2 = mybir.dt.float8_e5m2_x4
ACT = mybir.ActivationFunctionType
ALU = mybir.AluOpType

P = 128
PACK = 4
QUADRANTS = 4
LIVE_ROWS = 4
LIST_ROWS = 16
HALF = 128
HALVES = J // HALF
LIST_COLS = HALF // LIST_ROWS
RUNS = (slice(0, HALF // 2), slice(HALF // 2, HALF))
ODD = E // 2 + 1


def load_plane(queue, plane, scales):
    rows_per_quadrant = P // QUADRANTS
    for q in range(QUADRANTS):
        rows = scales[0, LIVE_ROWS * q : LIVE_ROWS * (q + 1), :].bitcast(I32)
        queue.dma_start(
            out=plane[rows_per_quadrant * q : rows_per_quadrant * (q + 1), :].bitcast(I32),
            in_=rows.unsqueeze(0).broadcast_to([rows_per_quadrant // LIVE_ROWS, LIVE_ROWS, rows.shape[1]]),
        )


def fp8_words(words):
    return words[0].rearrange("p n t -> p (n t)").bitcast(I32)


def tile_list_crossed_direct_one_scattered_kernel(
    tc, xt_words, xt_scales, xo_words, xo_scales, w_words, w_scales, w2_words, w2_scales,
    wb_words, wb_scales, offs, offs2, offs3, out,
):
    nc = tc.nc
    with ExitStack() as ctx:
        keep = ctx.enter_context(tc.tile_pool(name="keep", bufs=1))
        psum = ctx.enter_context(tc.psum_pool(name="psum", bufs=1))

        def tile(name, shape, dtype, tag=""):
            return keep.tile(shape, dtype, name=name, tag=tag, align_bytes=64)

        list_t = tile("list_t", [P, J // LIST_ROWS], U16)
        list_o = tile("list_o", [P, J // LIST_ROWS], U16)
        list_e = tile("list_e", [P, J // LIST_ROWS], U16)
        xt_w = tile("xt_w", [P, T], U16)
        xt_s = tile("xt_s", [P, T], U8)
        xo_w = tile("xo_w", [P, Z], U32)
        xo_s = tile("xo_s", [P, Z], U8)
        w_w = tile("w_w", [P, R], U32)
        w_s = tile("w_s", [P, R], U8)
        w2_w = tile("w2_w", [P, R], U32)
        w2_s = tile("w2_s", [P, R], U8)
        wb_w = tile("wb_w", [P, N], U32)
        wb_s = tile("wb_s", [P, N], U8)
        pages = [tile("page%d" % i, [P, E], F32) for i in range(N // P)]

        for page in pages:
            nc.vector.memset(page[:, :ODD], 0.0)
            nc.vector.memset(page[:, ODD:], 0.0)

        nc.gpsimd.dma_start(out=w_w[:].bitcast(I32), in_=fp8_words(w_words))
        nc.gpsimd.dma_start(out=w2_w[:].bitcast(I32), in_=fp8_words(w2_words))
        nc.gpsimd.dma_start(out=wb_w[:].bitcast(I32), in_=fp8_words(wb_words))
        nc.sync.dma_start(list_t[:], offs)
        load_plane(nc.sync, w_s, w_scales)
        nc.sync.dma_start(out=xt_w[:].bitcast(I32), in_=xt_words[0].bitcast(I32))
        load_plane(nc.sync, xt_s, xt_scales)
        nc.sync.dma_start(list_o[:], offs2)
        load_plane(nc.sync, w2_s, w2_scales)
        nc.sync.dma_start(out=xo_w[:].bitcast(I32), in_=fp8_words(xo_words))
        load_plane(nc.sync, xo_s, xo_scales)
        load_plane(nc.sync, wb_s, wb_scales)
        nc.sync.dma_start(list_e[:], offs3)

        def dealt(name, words, plane):
            words_d = tile(name + "_wd", [P, PACK, P], U32)
            plane_d = tile(name + "_sd", [P, PACK, P], U8)
            nc.vector.tensor_copy(
                out=plane_d[:].rearrange("p t (c i) -> p c t i", i=16),
                in_=plane[:].rearrange("p (c i t) -> p c t i", i=16, t=PACK),
            )
            nc.scalar.copy(
                out=words_d[:].rearrange("p t (c i) -> p c t i", i=4),
                in_=words[:].rearrange("p (c i t) -> p c t i", i=4, t=PACK),
            )
            return words_d, plane_d

        def entries(offsets, h):
            return offsets[:, h * LIST_COLS : (h + 1) * LIST_COLS]

        cols = [slice(h * HALF, (h + 1) * HALF) for h in range(HALVES)]
        gt_w = tile("gt_w", [P, J], U16)
        gt_s = tile("gt_s", [P, J], U8)
        go_s = [tile("go_s%d" % h, [P, HALF], U8) for h in range(HALVES)]
        w_wd, w_sd = dealt("w", w_w, w_s)
        nc.vector.tensor_copy(gt_w[:], xt_w[:].indirect(list_t[:]))
        nc.vector.tensor_copy(gt_s[:], xt_s[:].indirect(list_t[:]))
        w2_wd, w2_sd = dealt("w2", w2_w, w2_s)
        go_w = tile("go_w", [P, J], U32)
        nc.vector.tensor_copy(go_w[:], xo_w[:].indirect(list_o[:]))
        for h in range(HALVES):
            nc.vector.tensor_copy(go_s[h][:], xo_s[:].indirect(entries(list_o, h)))

        first = (w_wd, w_sd, E5M2)
        second = (w2_wd, w2_sd, E4M3)
        bank_a = [psum.tile([P, PACK, HALF], F32, name="bank_a%d" % h) for h in range(HALVES)]
        bank_b = [psum.tile([P, PACK, HALF], F32, name="bank_b%d" % h) for h in range(HALVES)]

        def passes(bank, weight, rhs, rhs_scale, opens):
            words_d, plane_d, fmt = weight
            for t in range(PACK):
                nc.tensor.matmul_mx(
                    out=bank[:, t, :],
                    lhsT=words_d[:, t, :].bitcast(fmt),
                    lhsT_scale=plane_d[:, t, :],
                    rhs=rhs,
                    rhs_scale=rhs_scale,
                    start=(opens and t == 0),
                    stop=(not opens and t == PACK - 1),
                )

        tokens = [(gt_w[:, c].bitcast(E2M1), gt_s[:, c]) for c in cols]
        notes = [(go_w[:, cols[h]].bitcast(E5M2), go_s[h][:]) for h in range(HALVES)]
        for banks, weight in ((bank_a, first), (bank_b, second)):
            for h in range(HALVES):
                passes(banks[h], weight, *tokens[h], True)
        for h in range(HALVES):
            for banks, weight in ((bank_b, first), (bank_a, second)):
                passes(banks[h], weight, *notes[h], False)

        hid_w, hid_s = [], []
        for h in range(HALVES):
            b_sb = tile("b_sb%d" % h, [P, HALF, PACK], F32)
            diff = tile("diff%d" % h, [P, HALF, PACK], F32, tag="diff%d" % h)
            hid = tile("hid%d" % h, [P, HALF, PACK], BF16, tag="hid%d" % h)
            hid_w.append(tile("hid_w%d" % h, [P, HALF], U32))
            hid_s.append(tile("hid_s%d" % h, [P, HALF], U8))
            for s in RUNS:
                nc.scalar.copy(out=b_sb[:, s, :], in_=bank_b[h][:, :, s].rearrange("p t j -> p j t"))
            for s in RUNS:
                nc.vector.tensor_tensor(
                    out=diff[:, s, :],
                    in0=bank_a[h][:, :, s].rearrange("p t j -> p j t"),
                    in1=b_sb[:, s, :],
                    op=ALU.subtract,
                )
                nc.scalar.activation(out=hid[:, s, :], in_=diff[:, s, :], func=ACT.Abs)
            nc.vector.quantize_mx(
                out=hid_w[h][:].bitcast(E5M2), scales=hid_s[h][:], in_=hid[:].rearrange("p j t -> p (j t)")
            )

        p_sb = [
            tile("p_sb0", [P, J], F32, tag="hid%d" % (HALVES - 1)),
            tile("p_sb1", [P, J], F32, tag="diff%d" % (HALVES - 1)),
        ]
        for h in range(HALVES):
            for i, page in enumerate(pages):
                n_cols = slice(i * P, (i + 1) * P)
                bank_p = psum.tile([P, HALF], F32, name="bank_p%d_%d" % (h, i))
                nc.tensor.matmul_mx(
                    out=bank_p[:],
                    lhsT=wb_w[:, n_cols].bitcast(E4M3),
                    lhsT_scale=wb_s[:, n_cols],
                    rhs=hid_w[h][:].bitcast(E5M2),
                    rhs_scale=hid_s[h][:],
                    start=True,
                    stop=True,
                )
                values = p_sb[i][:, cols[h]]
                places = page[:].indirect(entries(list_e, h))
                if i == 0:
                    nc.vector.tensor_copy(out=values, in_=bank_p[:])
                    nc.vector.tensor_copy(out=places, in_=values)
                else:
                    nc.scalar.copy(out=values, in_=bank_p[:])
                    nc.scalar.activation(out=places, in_=values, func=ACT.Copy)

        nc.sync.dma_start(out=out[0:P, :], in_=pages[0][:])
        nc.scalar.dma_start(out=out[P : 2 * P, :], in_=pages[1][:])
